import numpy as np, ml_dtypes
CORES = [56,64,184,192,312,320,440,448]
N = 8
KB, QP = 2, 512
MEM = [0]
WID = [64,512,64,512,320,512,64,448]
def setup_inputs(rng):
    return {"q": rng.standard_normal((N, 128, QP), dtype=np.float32).astype(ml_dtypes.bfloat16), "k": rng.standard_normal((N, 128, KB * 128), dtype=np.float32).astype(ml_dtypes.bfloat16), "v": rng.standard_normal((N, 128, KB * 128), dtype=np.float32).astype(ml_dtypes.bfloat16)}
def setup_inputs_big(rng):
    d = setup_inputs(rng)
    for k in ("q", "k", "v"): d[k] = (d[k].astype(np.float32) * 1024.0).astype(d[k].dtype)
    return d
def setup_inputs_small(rng):
    d = setup_inputs(rng)
    for k in ("q", "k", "v"): d[k] = (d[k].astype(np.float32) * (1 / 1024.0)).astype(d[k].dtype)
    return d
def setup_inputs_apart(rng):
    d = setup_inputs(rng)
    f = (10.0 ** rng.permutation(np.linspace(-1.5, 1.5, N))).astype(np.float32).reshape(N, 1, 1)
    for k in ("q", "k", "v"): d[k] = (d[k].astype(np.float32) * f).astype(d[k].dtype)
    return d
def whole(q, k, v):
    Q, K, V = q.astype(np.float64), k.astype(np.float64), v.astype(np.float64)
    y = np.zeros((N, 128, QP))
    for r in range(N):
        for j in MEM:
            for b in range(KB):
                S = np.maximum(K[j][:, 128 * b:128 * b + 128].T @ Q[r], 0.0)
                y[r] += V[j][:, 128 * b:128 * b + 128].T @ S
    return {"y": y.astype(ml_dtypes.bfloat16 if q.dtype != np.float64 else np.float64)}
def reference(q, k, v):
    o = whole(q, k, v)["y"].copy()
    for r in range(N):
        o[r][:, WID[r]:] = np.nan
    return {"y": o}

@@ -1,0 +1,199 @@
+from concourse.bass import DstId, RemoteDMATransfer
+from concourse.mybir import AluOpType
+
+WORLD = 512
+KB, BLK = 2, 128
+KW = KB * BLK
+
+E_OFF = 4
+E_ON = 8
+E_H = 8
+E_Q = 4
+
+SCRATCH = {
+    "kd": ("dram", [128, KW], "bfloat16"),
+    "vd": ("dram", [128, KW], "bfloat16"),
+    "kv": ("sbuf", [128, 2 * KW], "bfloat16"),
+    "qs": ("sbuf", [128, 512], "bfloat16"),
+    "zs": ("sbuf", [128, 512], "float32"),
+    "s0": ("sbuf", [128, 512], "bfloat16"),
+    "s1": ("sbuf", [128, 512], "bfloat16"),
+    "ysb": ("sbuf", [128, 512], "bfloat16"),
+    "ps0": ("psum", [128, 512], "float32"),
+    "ps1": ("psum", [128, 512], "float32"),
+    "po0": ("psum", [128, 512], "float32"),
+    "po1": ("psum", [128, 512], "float32"),
+}
+SEMAPHORES = ["kld", "vld", "qld", "qarr", "harr", "karr", "varr", "yarr", "sent", "zf",
+              "sm0", "sm1", "rl0", "rl1", "om0", "om1", "yc0", "yc1", "st0", "st1"]
+
+
+def _bits(mask):
+    return [1 << i for i in range(mask.bit_length()) if (mask >> i) & 1]
+
+
+def _join(bits):
+    m = 0
+    for b in bits:
+        m |= b
+    return m
+
+
+def _plan(T, topo):
+    cores, wid = list(T.cores), T.tables["WID"]
+    root = cores[T.tables["MEM"][0]]
+
+    def chip_of(x):
+        return [c for c in range(WORLD) if topo.host(c) == topo.host(x) and topo.chip(c) == topo.chip(x)]
+
+    def helpers(x, dests):
+        ok = [c for c in chip_of(x) if c not in cores and all(topo.may_write(c, d) for d in dests)]
+        return ([c for c in ok if topo.die(c) == topo.die(root)], [c for c in ok if topo.die(c) != topo.die(root)])
+
+    ship = [c for c in cores if c != root and wid[cores.index(c)] < KW
+            and topo.may_write(c, root) and topo.may_write(root, c)]
+    take = sorted([c for c in cores if c != root and c not in ship], key=lambda c: -wid[cores.index(c)])
+    direct = [d for d in take if any(topo.may_write(c, d) for c in chip_of(root))]
+    rest = [d for d in take if d not in direct]
+
+    sends = []
+    if direct:
+        same, other = helpers(root, direct)
+        for half, hs in (("k", other), ("v", same)):
+            n = min(len(hs), 2, len(direct))
+            step = -(-len(direct) // n)
+            for i in range(n):
+                sends.append((half, hs[i], direct[i * step:(i + 1) * step], True))
+    if rest:
+        gate = [c for c in cores if c != root and topo.may_write(root, c)
+                and topo.rack(topo.host(c)) == topo.rack(topo.host(rest[0]))][0]
+        same, other = helpers(gate, rest)
+        sends.append(("k", other[0], rest, False))
+        sends.append(("v", same[0], rest, False))
+    return root, ship, take, sends
+
+
+def _dst(topo, d, src):
+    rid, pid = topo.addr(d, src)
+    return DstId(rid=rid, pnc=pid)
+
+
+def _compute(g, T, width, qwaits, kn, vn, chunks):
+    s, te, ve = T.sem, g.tensor, g.vector
+    ve.memset(T.zs[:, 0:width], 0.0).then_inc(s.zf, 1)
+    for sem, n in qwaits:
+        te.wait_ge(sem, n)
+    te.wait_ge(s.karr, kn)
+    for b in range(KB):
+        te.matmul(T["ps%d" % b][:, 0:width], T.kv[:, b * BLK:(b + 1) * BLK], T.qs[:, 0:width],
+                  start=True, stop=True).then_inc(s["sm%d" % b], 1)
+    ve.wait_ge(s.zf, 1)
+    for b in range(KB):
+        ve.wait_ge(s["sm%d" % b], 1)
+        ve.tensor_tensor(T["s%d" % b][:, 0:width], T["ps%d" % b][:, 0:width], T.zs[:, 0:width],
+                         AluOpType.max).then_inc(s["rl%d" % b], 1)
+    te.wait_ge(s.varr, vn)
+    for b in range(KB):
+        te.wait_ge(s["rl%d" % b], 1)
+    for c, (a, z) in enumerate(chunks):
+        for b in range(KB):
+            mm = te.matmul(T["po%d" % c][:, 0:z - a], T.kv[:, KW + b * BLK:KW + (b + 1) * BLK], T["s%d" % b][:, a:z],
+                           start=(b == 0), stop=(b == KB - 1))
+        mm.then_inc(s["om%d" % c], 1)
+        ve.wait_ge(s["om%d" % c], 1)
+        ve.tensor_copy(T.ysb[:, a:z], T["po%d" % c][:, 0:z - a]).then_inc(s["yc%d" % c], 1)
+
+
+def _store(q, T, c, a, z):
+    q.wait_ge(T.sem["yc%d" % c], 1)
+    q.dma_start(T.y[:, a:z], T.ysb[:, a:z]).then_inc(T.sem["st%d" % c], 16)
+    q.wait_ge(T.sem["st%d" % c], 16)
+
+
+def rank_program(g, core, T, topo):
+    root, ship, take, sends = _plan(T, topo)
+    cores, wid, s = list(T.cores), T.tables["WID"], T.sem
+    road = {"k": T.kd, "v": T.vd}
+    home = {"k": T.kv[:, 0:KW], "v": T.kv[:, KW:2 * KW]}
+    here = {"k": s.karr, "v": s.varr}
+
+    if core == root:
+        w0 = wid[cores.index(root)]
+        g.sync.dma_start(T.kd[:], T.k[:]).then_inc(s.kld, 16)
+        g.scalar.dma_start(T.vd[:], T.v[:]).then_inc(s.vld, 16)
+        g.sync.dma_start(T.qs[:, 0:w0], T.q[:, 0:w0]).then_inc(s.qld, 16)
+        g.sync.dma_start(home["k"], T.k[:]).then_inc(s.karr, 16)
+        g.scalar.dma_start(home["v"], T.v[:]).then_inc(s.varr, 16)
+        far = [h for _, h, _, on in sends if not on]
+        off = _bits(topo.mask(root, far[0])) if far else []
+        near = [h for _, h, _, on in sends if on]
+        onb = [b for b in _bits(topo.mask(root, near[0])) if b not in off] if near else []
+        total = 0
+        for half, loaded in (("k", s.kld), ("v", s.vld)):
+            g.wait_ge(loaded, 16)
+            trs = []
+            hs = [h for p, h, _, on in sends if p == half and not on]
+            if hs:
+                trs.append(RemoteDMATransfer(dst_ids=[_dst(topo, h, root) for h in hs], dma_engine_mask=_join(off[:E_OFF]),
+                                             remote_sem=s.harr, srcs=[road[half][:]], dsts=[road[half][:] for h in hs]))
+                total += E_OFF
+            hs = [h for p, h, _, on in sends if p == half and on]
+            if hs:
+                trs.append(RemoteDMATransfer(dst_ids=[_dst(topo, h, root) for h in hs], dma_engine_mask=_join(onb[:E_ON]),
+                                             remote_sem=s.harr, srcs=[road[half][:]], dsts=[road[half][:] for h in hs]))
+                total += E_ON
+            g.remote_dma_fused(trs, local_sem=s.sent)
+        width = w0 + sum(wid[cores.index(c)] for c in ship)
+        chunks = [(w0, width), (0, w0)] if ship else [(0, w0)]
+        _compute(g, T, width, [(s.qld, 16)] + ([(s.qarr, E_Q * len(ship))] if ship else []), 16, 16, chunks)
+        _store(g.sync, T, len(chunks) - 1, 0, w0)
+        if ship:
+            g.wait_ge(s.yc0, 1)
+            a, back = w0, {}
+            for i, c in enumerate(ship):
+                w = wid[cores.index(c)]
+                eng = _bits(topo.mask(root, c))
+                eng = eng[(i * E_Q) % len(eng):][:E_Q]
+                back.setdefault(w, []).append(RemoteDMATransfer(
+                    dst_ids=[_dst(topo, c, root)], dma_engine_mask=_join(eng), remote_sem=s.yarr,
+                    srcs=[T.ysb[:, a:a + w]], dsts=[T.ysb[:, 0:w]]))
+                total += E_Q
+                a += w
+            for w in back:
+                g.remote_dma_fused(back[w], local_sem=s.sent)
+        g.wait_ge(s.sent, total)
+        return
+
+    if core in ship:
+        w = wid[cores.index(core)]
+        a = wid[cores.index(root)] + sum(wid[cores.index(c)] for c in ship[:ship.index(core)])
+        g.sync.dma_start(T.qs[:, 0:w], T.q[:, 0:w]).then_inc(s.qld, 16)
+        g.wait_ge(s.qld, 16)
+        rid, pid = topo.addr(root, core)
+        g.remote_dma(T.qs[:, a:a + w], T.qs[:, 0:w], s.qarr, s.sent, pid, rid, _join(_bits(topo.mask(core, root))[:E_Q]))
+        g.sync.wait_ge(s.yarr, E_Q)
+        g.sync.dma_start(T.y[:, 0:w], T.ysb[:, 0:w]).then_inc(s.st0, 16)
+        g.sync.wait_ge(s.st0, 16)
+        g.wait_ge(s.sent, E_Q)
+        return
+
+    if core in take:
+        w = wid[cores.index(core)]
+        g.sync.dma_start(T.qs[:, 0:w], T.q[:, 0:w]).then_inc(s.qld, 16)
+        h = (w // 2 + 7) // 8 * 8
+        _compute(g, T, w, [(s.qld, 16)], E_H, E_H, [(0, h), (h, w)])
+        _store(g.sync, T, 0, 0, h)
+        _store(g.scalar, T, 1, h, w)
+        return
+
+    for half, h, dests, on in sends:
+        if h == core:
+            eng = _bits(topo.mask(core, dests[0]))
+            for d in dests:
+                eng = [b for b in eng if b in _bits(topo.mask(core, d))]
+            g.wait_ge(s.harr, E_ON if on else E_OFF)
+            g.remote_dma_fused([RemoteDMATransfer(dst_ids=[_dst(topo, d, core) for d in dests],
+                                                  dma_engine_mask=_join(eng[:E_H]), remote_sem=here[half],
+                                                  srcs=[road[half][:]], dsts=[home[half] for d in dests])],
+                               local_sem=s.sent)
+            g.wait_ge(s.sent, E_H)

@@ -1,31 +1,34 @@
 from concourse.bass import DstId, RemoteDMATransfer
-from concourse.mybir import AluOpType
+from concourse.mybir import AluOpType, ActivationFunctionType
 
 WORLD = 512
 KB, BLK = 2, 128
 KW = KB * BLK
+PIECES = 4
+PW = KW // PIECES
 
-E_OFF = 4
-E_ON = 8
+E_P = 2
 E_H = 8
-E_Q = 4
+E_Q = 8
+E_Y = 4
 
 SCRATCH = {
-    "kd": ("dram", [128, KW], "bfloat16"),
-    "vd": ("dram", [128, KW], "bfloat16"),
+    "kd": ("dram", [PIECES, 128, PW], "bfloat16"),
+    "vd": ("dram", [PIECES, 128, PW], "bfloat16"),
     "kv": ("sbuf", [128, 2 * KW], "bfloat16"),
     "qs": ("sbuf", [128, 512], "bfloat16"),
-    "zs": ("sbuf", [128, 512], "float32"),
     "s0": ("sbuf", [128, 512], "bfloat16"),
     "s1": ("sbuf", [128, 512], "bfloat16"),
     "ysb": ("sbuf", [128, 512], "bfloat16"),
-    "ps0": ("psum", [128, 512], "float32"),
-    "ps1": ("psum", [128, 512], "float32"),
+    "ps00": ("psum", [128, 512], "float32"),
+    "ps10": ("psum", [128, 512], "float32"),
+    "ps01": ("psum", [128, 512], "float32"),
+    "ps11": ("psum", [128, 512], "float32"),
     "po0": ("psum", [128, 512], "float32"),
     "po1": ("psum", [128, 512], "float32"),
 }
-SEMAPHORES = ["kld", "vld", "qld", "qarr", "harr", "karr", "varr", "yarr", "sent", "zf",
-              "sm0", "sm1", "rl0", "rl1", "om0", "om1", "yc0", "yc1", "st0", "st1"]
+SEMAPHORES = ["kld", "vld", "qld", "qarr", "hk", "hv", "karr", "varr", "kin", "vin", "yarr", "sent",
+              "sm00", "sm10", "sm01", "sm11", "rl00", "rl10", "rl01", "rl11", "om0", "om1", "yc0", "yc1", "st0", "st1"]
 
 
 def _bits(mask):
@@ -37,6 +40,13 @@ def _join(bits):
     for b in bits:
         m |= b
     return m
+
+
+def _deal(bits):
+    out = [[] for _ in range(PIECES)]
+    for i, b in enumerate(bits[:E_P * PIECES]):
+        out[2 * (i // (2 * E_P)) + i % 2].append(b)
+    return [_join(x) for x in out]
 
 
 def _plan(T, topo):
@@ -56,21 +66,20 @@ def _plan(T, topo):
     direct = [d for d in take if any(topo.may_write(c, d) for c in chip_of(root))]
     rest = [d for d in take if d not in direct]
 
-    sends = []
+    groups = []
     if direct:
         same, other = helpers(root, direct)
-        for half, hs in (("k", other), ("v", same)):
-            n = min(len(hs), 2, len(direct))
-            step = -(-len(direct) // n)
-            for i in range(n):
-                sends.append((half, hs[i], direct[i * step:(i + 1) * step], True))
+        groups.append((direct, [same[0], other[0], same[1], other[1]], True))
     if rest:
-        gate = [c for c in cores if c != root and topo.may_write(root, c)
-                and topo.rack(topo.host(c)) == topo.rack(topo.host(rest[0]))][0]
-        same, other = helpers(gate, rest)
-        sends.append(("k", other[0], rest, False))
-        sends.append(("v", same[0], rest, False))
-    return root, ship, take, sends
+        gates = [c for c in cores if c != root and topo.may_write(root, c) and all(helpers(c, rest))]
+        gates.sort(key=lambda c: topo.rack(topo.host(c)) != topo.rack(topo.host(root)))
+        pools = [helpers(c, rest) for c in gates]
+        if len(pools) > 1:
+            hs = [pools[0][0][0], pools[1][0][0], pools[0][1][0], pools[1][1][0]]
+        else:
+            hs = [pools[0][0][0], pools[0][1][0], pools[0][0][1], pools[0][1][1]]
+        groups.append((rest, hs, False))
+    return root, ship, take, groups
 
 
 def _dst(topo, d, src):
@@ -78,25 +87,24 @@ def _dst(topo, d, src):
     return DstId(rid=rid, pnc=pid)
 
 
-def _compute(g, T, width, qwaits, kn, vn, chunks):
-    s, te, ve = T.sem, g.tensor, g.vector
-    ve.memset(T.zs[:, 0:width], 0.0).then_inc(s.zf, 1)
-    for sem, n in qwaits:
+def _compute(g, T, chunks, kwaits, vwaits):
+    s, te, ve, sc = T.sem, g.tensor, g.vector, g.scalar
+    for sem, n in kwaits:
         te.wait_ge(sem, n)
-    te.wait_ge(s.karr, kn)
-    for b in range(KB):
-        te.matmul(T["ps%d" % b][:, 0:width], T.kv[:, b * BLK:(b + 1) * BLK], T.qs[:, 0:width],
-                  start=True, stop=True).then_inc(s["sm%d" % b], 1)
-    ve.wait_ge(s.zf, 1)
-    for b in range(KB):
-        ve.wait_ge(s["sm%d" % b], 1)
-        ve.tensor_tensor(T["s%d" % b][:, 0:width], T["ps%d" % b][:, 0:width], T.zs[:, 0:width],
-                         AluOpType.max).then_inc(s["rl%d" % b], 1)
-    te.wait_ge(s.varr, vn)
-    for b in range(KB):
-        te.wait_ge(s["rl%d" % b], 1)
     for c, (a, z) in enumerate(chunks):
         for b in range(KB):
+            te.matmul(T["ps%d%d" % (b, c)][:, 0:z - a], T.kv[:, b * BLK:(b + 1) * BLK], T.qs[:, a:z],
+                      start=True, stop=True).then_inc(s["sm%d%d" % (b, c)], 1)
+    for c, (a, z) in enumerate(chunks):
+        ve.wait_ge(s["sm0%d" % c], 1)
+        ve.tensor_scalar(T.s0[:, a:z], T["ps0%d" % c][:, 0:z - a], 0.0, None, AluOpType.max).then_inc(s["rl0%d" % c], 1)
+        sc.wait_ge(s["sm1%d" % c], 1)
+        sc.activation(T.s1[:, a:z], T["ps1%d" % c][:, 0:z - a], ActivationFunctionType.Relu).then_inc(s["rl1%d" % c], 1)
+    for sem, n in vwaits:
+        te.wait_ge(sem, n)
+    for c, (a, z) in enumerate(chunks):
+        for b in range(KB):
+            te.wait_ge(s["rl%d%d" % (b, c)], 1)
             mm = te.matmul(T["po%d" % c][:, 0:z - a], T.kv[:, KW + b * BLK:KW + (b + 1) * BLK], T["s%d" % b][:, a:z],
                            start=(b == 0), stop=(b == KB - 1))
         mm.then_inc(s["om%d" % c], 1)
@@ -111,41 +119,35 @@ def _store(q, T, c, a, z):
 
 
 def rank_program(g, core, T, topo):
-    root, ship, take, sends = _plan(T, topo)
+    root, ship, take, groups = _plan(T, topo)
     cores, wid, s = list(T.cores), T.tables["WID"], T.sem
     road = {"k": T.kd, "v": T.vd}
-    home = {"k": T.kv[:, 0:KW], "v": T.kv[:, KW:2 * KW]}
-    here = {"k": s.karr, "v": s.varr}
 
     if core == root:
         w0 = wid[cores.index(root)]
         g.sync.dma_start(T.kd[:], T.k[:]).then_inc(s.kld, 16)
         g.scalar.dma_start(T.vd[:], T.v[:]).then_inc(s.vld, 16)
         g.sync.dma_start(T.qs[:, 0:w0], T.q[:, 0:w0]).then_inc(s.qld, 16)
-        g.sync.dma_start(home["k"], T.k[:]).then_inc(s.karr, 16)
-        g.scalar.dma_start(home["v"], T.v[:]).then_inc(s.varr, 16)
-        far = [h for _, h, _, on in sends if not on]
-        off = _bits(topo.mask(root, far[0])) if far else []
-        near = [h for _, h, _, on in sends if on]
-        onb = [b for b in _bits(topo.mask(root, near[0])) if b not in off] if near else []
+        g.sync.dma_start(T.kv[:, 0:KW], T.k[:]).then_inc(s.kin, 16)
+        g.scalar.dma_start(T.kv[:, KW:2 * KW], T.v[:]).then_inc(s.vin, 16)
+        off = []
+        for _, hs, on in groups:
+            if not on:
+                off = _bits(topo.mask(root, hs[0]))
         total = 0
-        for half, loaded in (("k", s.kld), ("v", s.vld)):
+        for half, loaded, there in (("k", s.kld, s.hk), ("v", s.vld, s.hv)):
             g.wait_ge(loaded, 16)
             trs = []
-            hs = [h for p, h, _, on in sends if p == half and not on]
-            if hs:
-                trs.append(RemoteDMATransfer(dst_ids=[_dst(topo, h, root) for h in hs], dma_engine_mask=_join(off[:E_OFF]),
-                                             remote_sem=s.harr, srcs=[road[half][:]], dsts=[road[half][:] for h in hs]))
-                total += E_OFF
-            hs = [h for p, h, _, on in sends if p == half and on]
-            if hs:
-                trs.append(RemoteDMATransfer(dst_ids=[_dst(topo, h, root) for h in hs], dma_engine_mask=_join(onb[:E_ON]),
-                                             remote_sem=s.harr, srcs=[road[half][:]], dsts=[road[half][:] for h in hs]))
-                total += E_ON
+            for _, hs, on in groups:
+                eng = [b for b in _bits(topo.mask(root, hs[0])) if b not in off] if on else off
+                for j, m in enumerate(_deal(eng)):
+                    trs.append(RemoteDMATransfer(dst_ids=[_dst(topo, hs[j], root)], dma_engine_mask=m, remote_sem=there,
+                                                 srcs=[road[half][j]], dsts=[road[half][j]]))
+                    total += E_P
             g.remote_dma_fused(trs, local_sem=s.sent)
         width = w0 + sum(wid[cores.index(c)] for c in ship)
         chunks = [(w0, width), (0, w0)] if ship else [(0, w0)]
-        _compute(g, T, width, [(s.qld, 16)] + ([(s.qarr, E_Q * len(ship))] if ship else []), 16, 16, chunks)
+        _compute(g, T, chunks, [(s.qld, 16), (s.kin, 16)] + ([(s.qarr, E_Q * len(ship))] if ship else []), [(s.vin, 16)])
         _store(g.sync, T, len(chunks) - 1, 0, w0)
         if ship:
             g.wait_ge(s.yc0, 1)
@@ -153,11 +155,11 @@ def rank_program(g, core, T, topo):
             for i, c in enumerate(ship):
                 w = wid[cores.index(c)]
                 eng = _bits(topo.mask(root, c))
-                eng = eng[(i * E_Q) % len(eng):][:E_Q]
+                eng = eng[(i * E_Y) % len(eng):][:E_Y]
                 back.setdefault(w, []).append(RemoteDMATransfer(
                     dst_ids=[_dst(topo, c, root)], dma_engine_mask=_join(eng), remote_sem=s.yarr,
                     srcs=[T.ysb[:, a:a + w]], dsts=[T.ysb[:, 0:w]]))
-                total += E_Q
+                total += E_Y
                 a += w
             for w in back:
                 g.remote_dma_fused(back[w], local_sem=s.sent)
@@ -171,7 +173,7 @@ def rank_program(g, core, T, topo):
         g.wait_ge(s.qld, 16)
         rid, pid = topo.addr(root, core)
         g.remote_dma(T.qs[:, a:a + w], T.qs[:, 0:w], s.qarr, s.sent, pid, rid, _join(_bits(topo.mask(core, root))[:E_Q]))
-        g.sync.wait_ge(s.yarr, E_Q)
+        g.sync.wait_ge(s.yarr, E_Y)
         g.sync.dma_start(T.y[:, 0:w], T.ysb[:, 0:w]).then_inc(s.st0, 16)
         g.sync.wait_ge(s.st0, 16)
         g.wait_ge(s.sent, E_Q)
@@ -180,20 +182,26 @@ def rank_program(g, core, T, topo):
     if core in take:
         w = wid[cores.index(core)]
         g.sync.dma_start(T.qs[:, 0:w], T.q[:, 0:w]).then_inc(s.qld, 16)
+        g.sync.wait_ge(s.karr, E_H * PIECES)
+        g.sync.dma_start(T.kv[:, 0:KW], T.kd[:]).then_inc(s.kin, 16)
+        g.sync.wait_ge(s.varr, E_H * PIECES)
+        g.sync.dma_start(T.kv[:, KW:2 * KW], T.vd[:]).then_inc(s.vin, 16)
         h = (w // 2 + 7) // 8 * 8
-        _compute(g, T, w, [(s.qld, 16)], E_H, E_H, [(0, h), (h, w)])
+        _compute(g, T, [(0, h), (h, w)], [(s.qld, 16), (s.kin, 16)], [(s.vin, 16)])
         _store(g.sync, T, 0, 0, h)
         _store(g.scalar, T, 1, h, w)
         return
 
-    for half, h, dests, on in sends:
-        if h == core:
+    for dests, hs, on in groups:
+        if core in hs:
+            j = hs.index(core)
             eng = _bits(topo.mask(core, dests[0]))
             for d in dests:
                 eng = [b for b in eng if b in _bits(topo.mask(core, d))]
-            g.wait_ge(s.harr, E_ON if on else E_OFF)
-            g.remote_dma_fused([RemoteDMATransfer(dst_ids=[_dst(topo, d, core) for d in dests],
-                                                  dma_engine_mask=_join(eng[:E_H]), remote_sem=here[half],
-                                                  srcs=[road[half][:]], dsts=[home[half] for d in dests])],
-                               local_sem=s.sent)
-            g.wait_ge(s.sent, E_H)
+            for half, got, there in (("k", s.hk, s.karr), ("v", s.hv, s.varr)):
+                g.wait_ge(got, E_P)
+                g.remote_dma_fused([RemoteDMATransfer(dst_ids=[_dst(topo, d, core) for d in dests],
+                                                      dma_engine_mask=_join(eng[:E_H]), remote_sem=there,
+                                                      srcs=[road[half][j]], dsts=[road[half][j] for d in dests])],
+                                   local_sem=s.sent)
+            g.wait_ge(s.sent, 2 * E_H)

from concourse.bass import DstId, RemoteDMATransfer
from concourse.mybir import AluOpType, ActivationFunctionType

WORLD = 512
KB, BLK = 2, 128
KW = KB * BLK
PIECES = 4
PW = KW // PIECES

E_P = 2
E_H = 8
E_Q = 8
E_Y = 4

SCRATCH = {
    "kd": ("dram", [PIECES, 128, PW], "bfloat16"),
    "vd": ("dram", [PIECES, 128, PW], "bfloat16"),
    "kv": ("sbuf", [128, 2 * KW], "bfloat16"),
    "qs": ("sbuf", [128, 512], "bfloat16"),
    "s0": ("sbuf", [128, 512], "bfloat16"),
    "s1": ("sbuf", [128, 512], "bfloat16"),
    "ysb": ("sbuf", [128, 512], "bfloat16"),
    "ps00": ("psum", [128, 512], "float32"),
    "ps10": ("psum", [128, 512], "float32"),
    "ps01": ("psum", [128, 512], "float32"),
    "ps11": ("psum", [128, 512], "float32"),
    "po0": ("psum", [128, 512], "float32"),
    "po1": ("psum", [128, 512], "float32"),
}
SEMAPHORES = ["kld", "vld", "qld", "qarr", "hk", "hv", "karr", "varr", "kin", "vin", "yarr", "sent",
              "sm00", "sm10", "sm01", "sm11", "rl00", "rl10", "rl01", "rl11", "om0", "om1", "yc0", "yc1", "st0", "st1"]


def _bits(mask):
    return [1 << i for i in range(mask.bit_length()) if (mask >> i) & 1]


def _join(bits):
    m = 0
    for b in bits:
        m |= b
    return m


def _deal(bits):
    out = [[] for _ in range(PIECES)]
    for i, b in enumerate(bits[:E_P * PIECES]):
        out[2 * (i // (2 * E_P)) + i % 2].append(b)
    return [_join(x) for x in out]


def _plan(T, topo):
    cores, wid = list(T.cores), T.tables["WID"]
    root = cores[T.tables["MEM"][0]]

    def chip_of(x):
        return [c for c in range(WORLD) if topo.host(c) == topo.host(x) and topo.chip(c) == topo.chip(x)]

    def helpers(x, dests):
        ok = [c for c in chip_of(x) if c not in cores and all(topo.may_write(c, d) for d in dests)]
        return ([c for c in ok if topo.die(c) == topo.die(root)], [c for c in ok if topo.die(c) != topo.die(root)])

    ship = [c for c in cores if c != root and wid[cores.index(c)] < KW
            and topo.may_write(c, root) and topo.may_write(root, c)]
    take = sorted([c for c in cores if c != root and c not in ship], key=lambda c: -wid[cores.index(c)])
    direct = [d for d in take if any(topo.may_write(c, d) for c in chip_of(root))]
    rest = [d for d in take if d not in direct]

    groups = []
    if direct:
        same, other = helpers(root, direct)
        groups.append((direct, [same[0], other[0], same[1], other[1]], True))
    if rest:
        gates = [c for c in cores if c != root and topo.may_write(root, c) and all(helpers(c, rest))]
        gates.sort(key=lambda c: topo.rack(topo.host(c)) != topo.rack(topo.host(root)))
        pools = [helpers(c, rest) for c in gates]
        if len(pools) > 1:
            hs = [pools[0][0][0], pools[1][0][0], pools[0][1][0], pools[1][1][0]]
        else:
            hs = [pools[0][0][0], pools[0][1][0], pools[0][0][1], pools[0][1][1]]
        groups.append((rest, hs, False))
    return root, ship, take, groups


def _dst(topo, d, src):
    rid, pid = topo.addr(d, src)
    return DstId(rid=rid, pnc=pid)


def _compute(g, T, chunks, kwaits, vwaits):
    s, te, ve, sc = T.sem, g.tensor, g.vector, g.scalar
    for sem, n in kwaits:
        te.wait_ge(sem, n)
    for c, (a, z) in enumerate(chunks):
        for b in range(KB):
            te.matmul(T["ps%d%d" % (b, c)][:, 0:z - a], T.kv[:, b * BLK:(b + 1) * BLK], T.qs[:, a:z],
                      start=True, stop=True).then_inc(s["sm%d%d" % (b, c)], 1)
    for c, (a, z) in enumerate(chunks):
        ve.wait_ge(s["sm0%d" % c], 1)
        ve.tensor_scalar(T.s0[:, a:z], T["ps0%d" % c][:, 0:z - a], 0.0, None, AluOpType.max).then_inc(s["rl0%d" % c], 1)
        sc.wait_ge(s["sm1%d" % c], 1)
        sc.activation(T.s1[:, a:z], T["ps1%d" % c][:, 0:z - a], ActivationFunctionType.Relu).then_inc(s["rl1%d" % c], 1)
    for sem, n in vwaits:
        te.wait_ge(sem, n)
    for c, (a, z) in enumerate(chunks):
        for b in range(KB):
            te.wait_ge(s["rl%d%d" % (b, c)], 1)
            mm = te.matmul(T["po%d" % c][:, 0:z - a], T.kv[:, KW + b * BLK:KW + (b + 1) * BLK], T["s%d" % b][:, a:z],
                           start=(b == 0), stop=(b == KB - 1))
        mm.then_inc(s["om%d" % c], 1)
        ve.wait_ge(s["om%d" % c], 1)
        ve.tensor_copy(T.ysb[:, a:z], T["po%d" % c][:, 0:z - a]).then_inc(s["yc%d" % c], 1)


def _store(q, T, c, a, z):
    q.wait_ge(T.sem["yc%d" % c], 1)
    q.dma_start(T.y[:, a:z], T.ysb[:, a:z]).then_inc(T.sem["st%d" % c], 16)
    q.wait_ge(T.sem["st%d" % c], 16)


def rank_program(g, core, T, topo):
    root, ship, take, groups = _plan(T, topo)
    cores, wid, s = list(T.cores), T.tables["WID"], T.sem
    road = {"k": T.kd, "v": T.vd}

    if core == root:
        w0 = wid[cores.index(root)]
        g.sync.dma_start(T.kd[:], T.k[:]).then_inc(s.kld, 16)
        g.scalar.dma_start(T.vd[:], T.v[:]).then_inc(s.vld, 16)
        g.sync.dma_start(T.qs[:, 0:w0], T.q[:, 0:w0]).then_inc(s.qld, 16)
        g.sync.dma_start(T.kv[:, 0:KW], T.k[:]).then_inc(s.kin, 16)
        g.scalar.dma_start(T.kv[:, KW:2 * KW], T.v[:]).then_inc(s.vin, 16)
        off = []
        for _, hs, on in groups:
            if not on:
                off = _bits(topo.mask(root, hs[0]))
        total = 0
        for half, loaded, there in (("k", s.kld, s.hk), ("v", s.vld, s.hv)):
            g.wait_ge(loaded, 16)
            trs = []
            for _, hs, on in groups:
                eng = [b for b in _bits(topo.mask(root, hs[0])) if b not in off] if on else off
                for j, m in enumerate(_deal(eng)):
                    trs.append(RemoteDMATransfer(dst_ids=[_dst(topo, hs[j], root)], dma_engine_mask=m, remote_sem=there,
                                                 srcs=[road[half][j]], dsts=[road[half][j]]))
                    total += E_P
            g.remote_dma_fused(trs, local_sem=s.sent)
        width = w0 + sum(wid[cores.index(c)] for c in ship)
        chunks = [(w0, width), (0, w0)] if ship else [(0, w0)]
        _compute(g, T, chunks, [(s.qld, 16), (s.kin, 16)] + ([(s.qarr, E_Q * len(ship))] if ship else []), [(s.vin, 16)])
        _store(g.sync, T, len(chunks) - 1, 0, w0)
        if ship:
            g.wait_ge(s.yc0, 1)
            a, back = w0, {}
            for i, c in enumerate(ship):
                w = wid[cores.index(c)]
                eng = _bits(topo.mask(root, c))
                eng = eng[(i * E_Y) % len(eng):][:E_Y]
                back.setdefault(w, []).append(RemoteDMATransfer(
                    dst_ids=[_dst(topo, c, root)], dma_engine_mask=_join(eng), remote_sem=s.yarr,
                    srcs=[T.ysb[:, a:a + w]], dsts=[T.ysb[:, 0:w]]))
                total += E_Y
                a += w
            for w in back:
                g.remote_dma_fused(back[w], local_sem=s.sent)
        g.wait_ge(s.sent, total)
        return

    if core in ship:
        w = wid[cores.index(core)]
        a = wid[cores.index(root)] + sum(wid[cores.index(c)] for c in ship[:ship.index(core)])
        g.sync.dma_start(T.qs[:, 0:w], T.q[:, 0:w]).then_inc(s.qld, 16)
        g.wait_ge(s.qld, 16)
        rid, pid = topo.addr(root, core)
        g.remote_dma(T.qs[:, a:a + w], T.qs[:, 0:w], s.qarr, s.sent, pid, rid, _join(_bits(topo.mask(core, root))[:E_Q]))
        g.sync.wait_ge(s.yarr, E_Y)
        g.sync.dma_start(T.y[:, 0:w], T.ysb[:, 0:w]).then_inc(s.st0, 16)
        g.sync.wait_ge(s.st0, 16)
        g.wait_ge(s.sent, E_Q)
        return

    if core in take:
        w = wid[cores.index(core)]
        g.sync.dma_start(T.qs[:, 0:w], T.q[:, 0:w]).then_inc(s.qld, 16)
        g.sync.wait_ge(s.karr, E_H * PIECES)
        g.sync.dma_start(T.kv[:, 0:KW], T.kd[:]).then_inc(s.kin, 16)
        g.sync.wait_ge(s.varr, E_H * PIECES)
        g.sync.dma_start(T.kv[:, KW:2 * KW], T.vd[:]).then_inc(s.vin, 16)
        h = (w // 2 + 7) // 8 * 8
        _compute(g, T, [(0, h), (h, w)], [(s.qld, 16), (s.kin, 16)], [(s.vin, 16)])
        _store(g.sync, T, 0, 0, h)
        _store(g.scalar, T, 1, h, w)
        return

    for dests, hs, on in groups:
        if core in hs:
            j = hs.index(core)
            eng = _bits(topo.mask(core, dests[0]))
            for d in dests:
                eng = [b for b in eng if b in _bits(topo.mask(core, d))]
            for half, got, there in (("k", s.hk, s.karr), ("v", s.hv, s.varr)):
                g.wait_ge(got, E_P)
                g.remote_dma_fused([RemoteDMATransfer(dst_ids=[_dst(topo, d, core) for d in dests],
                                                      dma_engine_mask=_join(eng[:E_H]), remote_sem=there,
                                                      srcs=[road[half][j]], dsts=[road[half][j] for d in dests])],
                                   local_sem=s.sent)
            g.wait_ge(s.sent, 2 * E_H)
